import numpy as np
import ml_dtypes


def mxq(x, axis, fmt="e4m3"):
    dtype, down = {"e4m3": (ml_dtypes.float8_e4m3fn, 7), "e5m2": (ml_dtypes.float8_e5m2, 14)}[fmt]
    v = np.moveaxis(np.asarray(x, np.float32).astype(ml_dtypes.bfloat16).astype(np.float64), axis, -1)
    blocks = v.reshape(v.shape[:-1] + (-1, 32))
    amax = np.abs(blocks).max(-1, keepdims=True)
    byte = np.maximum(np.where(amax > 0, np.frexp(amax)[1] - 1 + 127, 0) - down, 1)
    scale = np.exp2(byte - 127.0)
    codes = (blocks / scale).astype(np.float32).astype(dtype).astype(np.float64)
    return np.moveaxis((codes * scale).reshape(v.shape), -1, axis)


WIDE = False


def mx_kscale(k):
    if not WIDE:
        return np.ones(k)
    levels = np.array([10, -10, 5, -5, 0])
    if k % 512:
        return np.exp2(np.random.permutation(np.resize(levels, k // 32))).repeat(32)
    a = np.empty((k // 512, 16))
    for p in range(k // 512):
        a[p, :8] = np.random.permutation(np.resize(levels, 8))
        for g in range(8):
            far = levels[np.abs(levels - a[p, g]) >= 10]
            a[p, g + 8] = far[np.random.randint(len(far))]
    return np.exp2(a.ravel()).repeat(32)


def f64(x):
    return np.asarray(x).astype(np.float64)


def striped(idx):
    return np.tile(idx.reshape(-1, 16).T, (8, 1)).astype(np.uint16)


def unstriped(offs):
    return offs[:16].T.reshape(-1).astype(np.int64)


E2M1 = np.array([0.0, 0.5, 1.0, 1.5, 2.0, 3.0, 4.0, 6.0, -0.0, -0.5, -1.0, -1.5, -2.0, -3.0, -4.0, -6.0])


def pack_weight(w, fmt):
    k, n = w.shape
    w = f64(np.asarray(w, np.float32).astype(ml_dtypes.bfloat16)).reshape(k // 32, 32, n)
    amax = np.abs(w).max(1)
    if fmt == "e4m3":
        byte = np.frexp(amax)[1] - 1 + 127 - 7
    else:
        mant, ex = np.frexp(amax / 6.0)
        byte = np.where(mant > 0.5, ex, ex - 1) + 127
    byte = np.clip(np.where(amax > 0, byte, 1), 1, 254)
    scaled = (w * np.exp2(127.0 - byte)[:, None, :]).reshape(k, n).astype(np.float32)
    by_word = np.ascontiguousarray(scaled.reshape(k // 512, 128, 4, n).transpose(0, 1, 3, 2))
    if fmt == "e4m3":
        words = by_word.astype(ml_dtypes.float8_e4m3fn).view(np.uint8)
    else:
        c = by_word.astype(ml_dtypes.float4_e2m1fn).view(np.uint8) & 0xF
        words = (c[..., 0::2] | (c[..., 1::2] << 4)).reshape(k // 512, 128, 2 * n)
    return np.ascontiguousarray(words), np.ascontiguousarray(byte.astype(np.uint8).reshape(k // 512, 16, n))


def unpack_weight(words, scales, fmt):
    g, _, n = scales.shape
    words = np.ascontiguousarray(words).reshape(g, 128, n, -1)
    if fmt == "e4m3":
        vals = words.view(ml_dtypes.float8_e4m3fn).astype(np.float64)
    else:
        nib = np.empty((g, 128, n, 4), np.uint8)
        nib[..., 0::2] = words & 0xF
        nib[..., 1::2] = words >> 4
        vals = E2M1[nib]
    vals = vals * np.repeat(np.exp2(scales.astype(np.float64) - 127.0), 8, axis=1)[..., None]
    return vals.transpose(0, 1, 3, 2).reshape(g * 512, n)


def gelu(v):
    return 0.5 * v * (1.0 + np.tanh(np.sqrt(2.0 / np.pi) * (v + 0.044715 * v**3)))


K, H, T, S, T2, P = 1024, 1024, 2048, 1024, 2048, 512

def setup_inputs():
    n = np.random.standard_normal
    s = mx_kscale(K)[:, None]
    u = mx_kscale(H)[:, None]
    d = {}
    d["tab_words"], d["tab_scales"] = pack_weight(n((K, T)) * s, "e4m3")
    d["offs"] = striped(np.random.permutation(T)[:S])
    d["offs2"] = striped(np.random.permutation(T2)[:S])
    d["offs3"] = striped(np.random.permutation(T2)[:P])
    d["offs4"] = striped(np.random.permutation(T2)[:P])
    d["w1"] = (n((K, H)) / s * u.T / K ** 0.5).astype(np.float32)
    d["dive"] = (0.7 * n((H, S)) * u).astype(np.float32)
    d["wgs"] = np.exp(0.3 * n((128, S))).astype(np.float32)
    d["page0"] = (n((H, T2)) * u).astype(np.float32)
    d["gx"] = np.random.uniform(0.6, 1.6, H).astype(np.float32)
    d["w2_words"], d["w2_scales"] = pack_weight(1.2 * n((H, H)) / u / H ** 0.5, "e2m1")
    d["w3"] = (n((H, H)) / u / H ** 0.5).astype(np.float32)
    d["gb"] = (np.exp(0.3 * n(H)) / u[:, 0]).astype(np.float32)
    return d

def reference(tab_words, tab_scales, offs, offs2, offs3, offs4, w1, dive, wgs, page0, gx, w2_words, w2_scales, w3, gb):
    v = unpack_weight(tab_words, tab_scales, "e4m3")[:, unstriped(offs)]
    h = (mxq(f64(w1), 0, "e4m3").T @ v) + f64(dive)
    page = f64(page0).copy()
    page[:, unstriped(offs2)] = np.tile(f64(wgs), (H // 128, 1)) * h
    x = np.abs(page[:, unstriped(offs3)] * f64(gx)[:, None])
    xq = mxq(x, 0, "e4m3")
    p = unpack_weight(w2_words, w2_scales, "e2m1").T @ xq
    y = p / (1.0 + np.exp(-p))
    y2 = mxq(f64(w3), 0, "e4m3").T @ xq
    b = page[:, unstriped(offs4)] * f64(gb)[:, None]
    return y2 * b + y

@@ -1,0 +1,321 @@
+from contextlib import ExitStack
+
+import concourse.mybir as mybir
+from concourse.masks import make_identity
+
+FLOPS = 4294967296
+
+F32 = mybir.dt.float32
+BF16 = mybir.dt.bfloat16
+I32 = mybir.dt.int32
+U32 = mybir.dt.uint32
+U16 = mybir.dt.uint16
+U8 = mybir.dt.uint8
+FP8X4 = mybir.dt.float8_e4m3fn_x4
+FP4X4 = mybir.dt.float4_e2m1fn_x4
+ACT = mybir.ActivationFunctionType
+MULT = mybir.AluOpType.mult
+ADD = mybir.AluOpType.add
+
+P = 128
+PACK = 4
+BANK = 512
+PASSES = 2
+TILES = 8
+T = 2048
+S = 1024
+PICKS = 512
+EARLY = 3
+
+
+def tile_list_tissue_page_features_kernel(
+    tc, tab_words, tab_scales, offs, offs2, offs3, offs4, w1, dive, wgs, page0, gx, w2_words, w2_scales, w3, gb, out
+):
+    nc = tc.nc
+    with ExitStack() as ctx:
+        keep = ctx.enter_context(tc.tile_pool(name="keep", bufs=1))
+        ring = ctx.enter_context(tc.tile_pool(name="ring", bufs=2))
+        psum = ctx.enter_context(tc.psum_pool(name="psum", bufs=1))
+
+        def dealt(x):
+            return x.rearrange("(b p t) c -> b t p c", p=P, t=PACK)
+
+        def bank(tag):
+            return psum.tile([P, BANK], F32, name=tag, tag=tag)
+
+        tab_s = keep.tile([P, T], U8, name="tab_s")
+        nc.gpsimd.memset(tab_s[:].bitcast(I32), 0)
+        w2_s = keep.tile([P, PASSES, 1024], U8, name="w2_s", align_bytes=64)
+        nc.gpsimd.memset(w2_s[:].rearrange("p a c -> p (a c)").bitcast(I32), 0)
+        warm = keep.tile([P, 8], F32, name="warm")
+        nc.gpsimd.memset(warm[:], 0.0)
+        warm_out = keep.tile([P, 8], F32, name="warm_out")
+        nc.scalar.activation(warm_out[:], warm[:], ACT.Silu)
+        ident = keep.tile([P, P], F32, name="ident")
+        make_identity(nc, ident[:])
+
+        def load_list(x, name):
+            t = keep.tile([P, x.shape[1]], U16, name=name)
+            nc.sync.dma_start(t[:], x)
+            return t
+
+        def load_table(a):
+            t = keep.tile([P, T], I32, name="tab%d" % a, tag="tab%d" % a)
+            nc.sync.dma_start(t[:], tab_words[a].rearrange("p t i -> p (t i)").bitcast(I32))
+            return t
+
+        def load_weight(w, a, b):
+            raw = ring.tile([P, PACK, BANK], F32, name="raw", tag="raw", bufs=3)
+            rows = w[BANK * a : BANK * (a + 1), BANK * b : BANK * (b + 1)]
+            nc.sync.dma_start(raw[:], rows.rearrange("(p j) c -> p j c", j=PACK))
+            return raw
+
+        def quantize(grouped, name):
+            codes = keep.tile([P, BANK], U32, name=name + "_c", align_bytes=64)
+            scales = keep.tile([P, BANK], U8, name=name + "_s", align_bytes=64)
+            nc.vector.quantize_mx(out=codes[:].bitcast(FP8X4), scales=scales[:], in_=grouped[:])
+            return codes, scales
+
+        def quantize_weight(raw, name):
+            grouped = ring.tile([P, PACK * BANK], BF16, name="grouped", tag="grouped", align_bytes=64)
+            nc.scalar.copy(
+                grouped[:].rearrange("p (t m j) -> p m j t", t=PACK, j=PACK),
+                raw[:].rearrange("p j (m t) -> p m j t", t=PACK),
+            )
+            return quantize(grouped, name)
+
+        pages, dives, gains = {}, {}, {}
+
+        def load_tile(i):
+            b, t = divmod(i, PACK)
+            dives[i] = ring.tile([P, S], F32, name="dive", tag="dive", bufs=3)
+            nc.sync.dma_start(dives[i][:], dealt(dive)[b, t])
+            if b == 0:
+                gains[t] = keep.tile([P, S], F32, name="gain%d" % t, tag="gain%d" % t)
+                for g in range(4):
+                    nc.sync.dma_start(
+                        gains[t][32 * g : 32 * (g + 1), :], wgs.rearrange("(q t) j -> t q j", t=PACK)[t]
+                    )
+            pages[i] = keep.tile([P, T], F32, name="page%d" % i)
+            nc.sync.dma_start(pages[i][:], dealt(page0)[b, t])
+
+        idx = load_list(offs, "idx")
+        tabs = [load_table(0)]
+        for q in range(4):
+            nc.sync.dma_start(
+                tab_s[32 * q : 32 * q + 8, :].bitcast(I32), tab_scales[:, 4 * q : 4 * q + 4, :].bitcast(I32)
+            )
+        tabs.append(load_table(1))
+        raws = [load_weight(w1, a, 0) for a in range(PASSES)]
+        idx2 = load_list(offs2, "idx2")
+        load_tile(0)
+
+        v_c = []
+        for a in range(PASSES):
+            v_c.append(keep.tile([P, S], U32, name="v_c%d" % a, align_bytes=64))
+            nc.vector.tensor_copy(v_c[a][:], tabs[a][:].bitcast(U32).indirect(idx[:]))
+        v_s = keep.tile([P, S], U8, name="v_s", align_bytes=64)
+        nc.vector.tensor_copy(v_s[:], tab_s[:].indirect(idx[:]))
+
+        w1q, w3q = {}, {}
+        for a in range(PASSES):
+            w1q[a, 0] = quantize_weight(raws[a], "w1_%d0" % a)
+
+        def first_product(i, half):
+            b, t = divmod(i, PACK)
+            acc = bank("A%d" % half)
+            cols = slice(BANK * half, BANK * (half + 1))
+            rows = slice(P * t, P * (t + 1))
+            for a in range(PASSES):
+                codes, scales = w1q[a, b]
+                nc.tensor.matmul_mx(
+                    out=acc[:],
+                    lhsT=codes[:, rows].bitcast(FP8X4),
+                    lhsT_scale=scales[:, rows],
+                    rhs=v_c[a][:, cols].bitcast(FP8X4),
+                    rhs_scale=v_s[4 * a : P, cols],
+                    start=(a == 0),
+                    stop=(a == PASSES - 1),
+                )
+            return acc
+
+        def add_on_tensor(i, half, h):
+            acc = first_product(i, half)
+            prod = ring.tile([P, BANK], F32, name="prod", tag="prod")
+            nc.scalar.copy(prod[:], acc[:])
+            turned = bank("B%d" % half)
+            sources = [dives[i][:, BANK * half : BANK * (half + 1)], prod[:]]
+            for s in range(2):
+                for k in range(4):
+                    nc.tensor.matmul(
+                        turned[:, P * k : P * (k + 1)],
+                        lhsT=sources[s][:, P * k : P * (k + 1)],
+                        rhs=ident[:],
+                        is_transpose=True,
+                        start=(s == 0 and k == 0),
+                        stop=(s == 1 and k == 3),
+                    )
+            tag = "hT%d%d" % (half, i % 2)
+            h_t = keep.tile([P, BANK], F32, name=tag, tag=tag)
+            nc.scalar.copy(h_t[:], turned[:])
+            back = bank("C%d" % half)
+            for k in range(4):
+                nc.tensor.transpose(back[:, P * k : P * (k + 1)], h_t[:, P * k : P * (k + 1)], ident[:])
+            nc.scalar.copy(h[:, BANK * half : BANK * (half + 1)], back[:])
+
+        x_b = [keep.tile([P, PICKS, PACK], BF16, name="x_b%d" % a, align_bytes=64) for a in range(PASSES)]
+        xq = {}
+
+        def pick_x(tiles, tag):
+            got = keep.tile([P, len(tiles), PICKS], F32, name="got", tag=tag)
+            for n, i in enumerate(tiles):
+                nc.vector.tensor_copy(got[:, n, :], pages[i][:].indirect(idx3[:]))
+            for n, i in enumerate(tiles):
+                b, t = divmod(i, PACK)
+                nc.scalar.activation(x_b[b][:, :, t], got[:, n, :], ACT.Abs, scale=gx_t[:, b, t : t + 1])
+                if t == PACK - 1:
+                    xq[b] = quantize(x_b[b][:].rearrange("p m t -> p (m t)"), "x%d" % b)
+
+        hs = {}
+        for i in range(TILES):
+            b, t = divmod(i, PACK)
+            hs[i] = keep.tile([P, S], F32, name="h", tag="h%d" % (i % 2))
+            if i == 0:
+                for half in range(2):
+                    cols = slice(BANK * half, BANK * (half + 1))
+                    acc = first_product(i, half)
+                    nc.vector.tensor_tensor(hs[i][:, cols], acc[:], dives[i][:, cols], ADD)
+                for half in range(2):
+                    cols = slice(BANK * half, BANK * (half + 1))
+                    nc.vector.tensor_tensor(
+                        pages[i][:].indirect(idx2[:, 32 * half : 32 * (half + 1)]),
+                        hs[i][:, cols],
+                        gains[t][:, cols],
+                        MULT,
+                    )
+            else:
+                for half in range(2):
+                    add_on_tensor(i, half, hs[i])
+                if i >= 2:
+                    pick_x([i - 2] if i < TILES - 1 else [i - 2, i - 1], "hT1%d" % (i % 2))
+                nc.vector.tensor_tensor(pages[i][:].indirect(idx2[:]), hs[i][:], gains[t][:], MULT)
+            if i + 1 < TILES:
+                load_tile(i + 1)
+            if i == 0:
+                idx3 = load_list(offs3, "idx3")
+                idx4 = load_list(offs4, "idx4")
+                gx_t = keep.tile([P, PASSES, PACK], F32, name="gx_t")
+                nc.sync.dma_start(gx_t[:], gx.rearrange("(b p t) -> p b t", p=P, t=PACK))
+                gb_t = keep.tile([P, PASSES, PACK], F32, name="gb_t")
+                nc.sync.dma_start(gb_t[:], gb.rearrange("(b p t) -> p b t", p=P, t=PACK))
+                for a in range(PASSES):
+                    w1q[a, 1] = quantize_weight(load_weight(w1, a, 1), "w1_%d1" % a)
+            if 3 <= i <= 6:
+                bb, a = divmod(i - 3, PASSES)
+                w3q[a, bb] = quantize_weight(load_weight(w3, a, bb), "w3_%d%d" % (a, bb))
+            if i == 4:
+                w2_c = keep.tile([P, PASSES, 2048], U8, name="w2_c", align_bytes=64)
+                nc.sync.dma_start(w2_c[:].bitcast(I32), w2_words.rearrange("a p c -> p a c").bitcast(I32))
+                for q in range(4):
+                    nc.sync.dma_start(
+                        w2_s[32 * q : 32 * q + 4, :, :].bitcast(I32),
+                        w2_scales[:, 4 * q : 4 * q + 4, :].rearrange("a r c -> r a c").bitcast(I32),
+                    )
+
+        def y2_pass(acc, i, a):
+            b, t = divmod(i, PACK)
+            codes, scales = w3q[a, b]
+            rows = slice(P * t, P * (t + 1))
+            nc.tensor.matmul_mx(
+                out=acc[:],
+                lhsT=codes[:, rows].bitcast(FP8X4),
+                lhsT_scale=scales[:, rows],
+                rhs=xq[a][0][:].bitcast(FP8X4),
+                rhs_scale=xq[a][1][:],
+                start=(a == 0),
+                stop=(a == PASSES - 1),
+            )
+
+        def p_pass(acc, b, mb, a):
+            cols = slice(P * mb, P * (mb + 1))
+            nc.tensor.matmul_mx(
+                out=acc[:],
+                lhsT=xq[a][0][:, cols].bitcast(FP8X4),
+                lhsT_scale=xq[a][1][:, cols],
+                rhs=w2_c[:, a, 2 * BANK * b : 2 * BANK * (b + 1)].bitcast(FP4X4),
+                rhs_scale=w2_s[:, a, BANK * b : BANK * (b + 1)],
+                start=(a == 0),
+                stop=(a == PASSES - 1),
+            )
+
+        y2_tags = ["A0", "A1", "B0", "B1"]
+        y2 = {}
+        for i in range(4):
+            y2[i] = bank(y2_tags[i])
+            y2_pass(y2[i], i, 0)
+        pt = {}
+        for mb in range(2):
+            pt[0, mb] = bank("C%d" % mb)
+            p_pass(pt[0, mb], 0, mb, 0)
+
+        pick_x([TILES - 1], "hT10")
+        early_a = keep.tile([P, 2, PICKS], F32, name="early_a", tag="gain3")
+        early_b = keep.tile([P, 2, PICKS], F32, name="early_b", tag="h1")
+        early = [early_a[:, 0, :], early_a[:, 1, :], early_b[:, 0, :], early_b[:, 1, :]]
+        for i in range(EARLY):
+            nc.vector.tensor_copy(early[i], pages[i][:].indirect(idx4[:]))
+
+        z = {}
+
+        def buddy(i):
+            b, t = divmod(i, PACK)
+            z[i] = ring.tile([P, PICKS], F32, name="z", tag="z", bufs=6)
+            if i < EARLY:
+                nc.vector.scalar_tensor_tensor(z[i][:], y2[i][:], gb_t[:, b, t : t + 1], early[i], MULT, MULT)
+            else:
+                scaled = ring.tile([P, PICKS], F32, name="scaled", tag="dive", bufs=3)
+                nc.scalar.activation(scaled[:], y2[i][:], ACT.Copy, scale=gb_t[:, b, t : t + 1])
+                nc.vector.tensor_tensor(z[i][:], pages[i][:].indirect(idx4[:]), scaled[:], MULT)
+
+        y_t = [keep.tile([P, 4, PACK, P], F32, name="y_t%d" % b, tag="tab%d" % b) for b in range(2)]
+
+        def silu(b, mb):
+            nc.scalar.activation(y_t[b][:, mb, :, :], pt[b, mb][:].rearrange("p (q t) -> p t q", t=PACK), ACT.Silu)
+
+        def p_whole(b, mb):
+            pt[b, mb] = bank("C%d" % (mb % 2))
+            for a in range(PASSES):
+                p_pass(pt[b, mb], b, mb, a)
+            silu(b, mb)
+
+        def y2_whole(i):
+            y2[i] = bank(y2_tags[i % 4])
+            for a in range(PASSES):
+                y2_pass(y2[i], i, a)
+            buddy(i)
+
+        def finish(i):
+            b, t = divmod(i, PACK)
+            y = bank("D%d" % (i % 2))
+            for mb in range(4):
+                nc.tensor.transpose(y[:, P * mb : P * (mb + 1)], y_t[b][:, mb, t, :], ident[:])
+            nc.vector.tensor_tensor(z[i][:], y[:], z[i][:], ADD)
+            nc.sync.dma_start(dealt(out)[b, t], z[i][:])
+
+        for i in range(4):
+            y2_pass(y2[i], i, 1)
+            buddy(i)
+        for mb in range(2):
+            p_pass(pt[0, mb], 0, mb, 1)
+            silu(0, mb)
+        for mb in range(2, 4):
+            p_whole(0, mb)
+        for i in range(4, 6):
+            y2_whole(i)
+        for mb in range(4):
+            p_whole(1, mb)
+            finish(mb)
+            if mb < 2:
+                y2_whole(6 + mb)
+        for i in range(4, TILES):
+            finish(i)

@@ -25,7 +25,8 @@ TILES = 8
 T = 2048
 S = 1024
 PICKS = 512
-EARLY = 3
+WIDE = 256
+EARLY = 4
 
 
 def tile_list_tissue_page_features_kernel(
@@ -34,25 +35,29 @@ def tile_list_tissue_page_features_kernel(
     nc = tc.nc
     with ExitStack() as ctx:
         keep = ctx.enter_context(tc.tile_pool(name="keep", bufs=1))
-        ring = ctx.enter_context(tc.tile_pool(name="ring", bufs=2))
+        ring = ctx.enter_context(tc.tile_pool(name="ring", bufs=3))
         psum = ctx.enter_context(tc.psum_pool(name="psum", bufs=1))
 
-        def dealt(x):
-            return x.rearrange("(b p t) c -> b t p c", p=P, t=PACK)
+        halves = [slice(BANK * n, BANK * (n + 1)) for n in range(2)]
+        blocks = [slice(P * n, P * (n + 1)) for n in range(TILES)]
 
-        def bank(tag):
-            return psum.tile([P, BANK], F32, name=tag, tag=tag)
+        def bank(tag, dtype=F32):
+            return psum.tile([P, BANK], dtype, name=tag, tag=tag)
 
         tab_s = keep.tile([P, T], U8, name="tab_s")
         nc.gpsimd.memset(tab_s[:].bitcast(I32), 0)
-        w2_s = keep.tile([P, PASSES, 1024], U8, name="w2_s", align_bytes=64)
-        nc.gpsimd.memset(w2_s[:].rearrange("p a c -> p (a c)").bitcast(I32), 0)
         warm = keep.tile([P, 8], F32, name="warm")
         nc.gpsimd.memset(warm[:], 0.0)
         warm_out = keep.tile([P, 8], F32, name="warm_out")
         nc.scalar.activation(warm_out[:], warm[:], ACT.Silu)
+        w2_s = keep.tile([P, PASSES, 1024], U8, name="w2_s", align_bytes=64)
+        nc.gpsimd.memset(w2_s[:].rearrange("p a c -> p (a c)").bitcast(I32), 0)
+        factor_rows = keep.tile([P, P], F32, name="factor_rows")
+        nc.gpsimd.memset(factor_rows[:], 0.0)
         ident = keep.tile([P, P], F32, name="ident")
         make_identity(nc, ident[:])
+        ident_b = keep.tile([P, P], BF16, name="ident_b")
+        make_identity(nc, ident_b[:])
 
         def load_list(x, name):
             t = keep.tile([P, x.shape[1]], U16, name=name)
@@ -64,40 +69,53 @@ def tile_list_tissue_page_features_kernel(
             nc.sync.dma_start(t[:], tab_words[a].rearrange("p t i -> p (t i)").bitcast(I32))
             return t
 
-        def load_weight(w, a, b):
-            raw = ring.tile([P, PACK, BANK], F32, name="raw", tag="raw", bufs=3)
-            rows = w[BANK * a : BANK * (a + 1), BANK * b : BANK * (b + 1)]
-            nc.sync.dma_start(raw[:], rows.rearrange("(p j) c -> p j c", j=PACK))
-            return raw
+        def raw_tile():
+            return ring.tile([P, PASSES, PACK, WIDE], F32, name="raw", tag="raw")
 
-        def quantize(grouped, name):
-            codes = keep.tile([P, BANK], U32, name=name + "_c", align_bytes=64)
+        def load_weight(raw, w, g, a):
+            rows = w[BANK * a : BANK * (a + 1), WIDE * g : WIDE * (g + 1)]
+            nc.sync.dma_start(raw[:, a, :, :], rows.rearrange("(p j) c -> p j c", j=PACK))
+
+        def grouped_tile():
+            return ring.tile([P, PACK * BANK], BF16, name="grouped", tag="grouped", align_bytes=64)
+
+        def round_weight(grouped, raw, a):
+            dst = grouped[:].rearrange("p (a c i j) -> p a c j i", a=PASSES, i=4, j=PACK)
+            src = raw[:].rearrange("p a j (c i) -> p a c j i", i=4)
+            nc.scalar.copy(dst[:, a, :, :, :], src[:, a, :, :, :])
+
+        def quantize(grouped, name, codes=None):
+            if codes is None:
+                codes = keep.tile([P, BANK], U32, name=name + "_c", align_bytes=64)[:]
             scales = keep.tile([P, BANK], U8, name=name + "_s", align_bytes=64)
-            nc.vector.quantize_mx(out=codes[:].bitcast(FP8X4), scales=scales[:], in_=grouped[:])
+            nc.vector.quantize_mx(out=codes.bitcast(FP8X4), scales=scales[:], in_=grouped[:])
             return codes, scales
 
-        def quantize_weight(raw, name):
-            grouped = ring.tile([P, PACK * BANK], BF16, name="grouped", tag="grouped", align_bytes=64)
-            nc.scalar.copy(
-                grouped[:].rearrange("p (t m j) -> p m j t", t=PACK, j=PACK),
-                raw[:].rearrange("p j (m t) -> p m j t", t=PACK),
-            )
-            return quantize(grouped, name)
+        def weight_columns(q, i, a):
+            codes, scales = q[i // 2]
+            cols = slice(WIDE * a + P * (i % 2), WIDE * a + P * (i % 2 + 1))
+            return codes[:, cols].bitcast(FP8X4), scales[:, cols]
 
-        pages, dives, gains = {}, {}, {}
+        pages, dives, waiting = {}, {}, {}
+        plan = {1: (w1, 1), 3: (w1, 2), 4: (w1, 3), 5: (w3, 0), 6: (w3, 1), 7: (w3, 2), 8: (w3, 3)}
 
         def load_tile(i):
-            b, t = divmod(i, PACK)
-            dives[i] = ring.tile([P, S], F32, name="dive", tag="dive", bufs=3)
-            nc.sync.dma_start(dives[i][:], dealt(dive)[b, t])
-            if b == 0:
-                gains[t] = keep.tile([P, S], F32, name="gain%d" % t, tag="gain%d" % t)
-                for g in range(4):
-                    nc.sync.dma_start(
-                        gains[t][32 * g : 32 * (g + 1), :], wgs.rearrange("(q t) j -> t q j", t=PACK)[t]
-                    )
+            early = i in plan and i < 5
+            if early:
+                waiting[i] = raw_tile()
+                load_weight(waiting[i], w1, plan[i][1], 0)
+            dives[i] = ring.tile([P, S], F32, name="dive", tag="dive")
+            nc.sync.dma_start(dives[i][:], dive[blocks[i], :])
+            if early:
+                load_weight(waiting[i], w1, plan[i][1], 1)
+            if i == 0:
+                nc.sync.dma_start(gain[:], wgs)
             pages[i] = keep.tile([P, T], F32, name="page%d" % i)
-            nc.sync.dma_start(pages[i][:], dealt(page0)[b, t])
+            nc.sync.dma_start(pages[i][:], page0[blocks[i], :])
+            if i >= 4:
+                waiting[i + 1] = raw_tile()
+                for a in range(PASSES):
+                    load_weight(waiting[i + 1], w3, i - 4, a)
 
         idx = load_list(offs, "idx")
         tabs = [load_table(0)]
@@ -105,115 +123,135 @@ def tile_list_tissue_page_features_kernel(
             nc.sync.dma_start(
                 tab_s[32 * q : 32 * q + 8, :].bitcast(I32), tab_scales[:, 4 * q : 4 * q + 4, :].bitcast(I32)
             )
+        raw = raw_tile()
+        for a in range(PASSES):
+            load_weight(raw, w1, 0, a)
         tabs.append(load_table(1))
-        raws = [load_weight(w1, a, 0) for a in range(PASSES)]
         idx2 = load_list(offs2, "idx2")
+        gain = keep.tile([P, S], F32, name="gain", tag="gain")
         load_tile(0)
 
-        v_c = []
-        for a in range(PASSES):
-            v_c.append(keep.tile([P, S], U32, name="v_c%d" % a, align_bytes=64))
-            nc.vector.tensor_copy(v_c[a][:], tabs[a][:].bitcast(U32).indirect(idx[:]))
+        v_c = [keep.tile([P, S], U32, name="v_c%d" % a, align_bytes=64) for a in range(PASSES)]
         v_s = keep.tile([P, S], U8, name="v_s", align_bytes=64)
-        nc.vector.tensor_copy(v_s[:], tab_s[:].indirect(idx[:]))
-
         w1q, w3q = {}, {}
+        nc.vector.tensor_copy(v_c[0][:], tabs[0][:].bitcast(U32).indirect(idx[:]))
+        nc.vector.tensor_copy(v_s[:], tab_s[:].indirect(idx[:]))
+        grouped = grouped_tile()
         for a in range(PASSES):
-            w1q[a, 0] = quantize_weight(raws[a], "w1_%d0" % a)
+            round_weight(grouped, raw, a)
+        w1q[0] = quantize(grouped, "w1_0")
+        for half in range(2):
+            nc.vector.tensor_copy(
+                v_c[1][:, halves[half]], tabs[1][:].bitcast(U32).indirect(idx[:, 32 * half : 32 * (half + 1)])
+            )
 
         def first_product(i, half):
-            b, t = divmod(i, PACK)
-            acc = bank("A%d" % half)
-            cols = slice(BANK * half, BANK * (half + 1))
-            rows = slice(P * t, P * (t + 1))
+            acc = bank(("A%d" if i > 0 else "C%d") % half)
             for a in range(PASSES):
-                codes, scales = w1q[a, b]
+                codes, scales = weight_columns(w1q, i, a)
                 nc.tensor.matmul_mx(
                     out=acc[:],
-                    lhsT=codes[:, rows].bitcast(FP8X4),
-                    lhsT_scale=scales[:, rows],
-                    rhs=v_c[a][:, cols].bitcast(FP8X4),
-                    rhs_scale=v_s[4 * a : P, cols],
+                    lhsT=codes,
+                    lhsT_scale=scales,
+                    rhs=v_c[a][:, halves[half]].bitcast(FP8X4),
+                    rhs_scale=v_s[4 * a : P, halves[half]],
                     start=(a == 0),
                     stop=(a == PASSES - 1),
                 )
             return acc
 
-        def add_on_tensor(i, half, h):
-            acc = first_product(i, half)
-            prod = ring.tile([P, BANK], F32, name="prod", tag="prod")
-            nc.scalar.copy(prod[:], acc[:])
-            turned = bank("B%d" % half)
-            sources = [dives[i][:, BANK * half : BANK * (half + 1)], prod[:]]
-            for s in range(2):
+        def add_on_tensor(i, h):
+            turned, back = [], []
+            for half in range(2):
+                acc = first_product(i, half)
+                prod = ring.tile([P, BANK], F32, name="prod", tag="prod", bufs=2)
+                nc.scalar.copy(prod[:], acc[:])
+                turned.append(bank(["B0", "B1", "D1"][(2 * i + half) % 3]))
+                for s, source in enumerate([dives[i][:, halves[half]], prod[:]]):
+                    for k in range(4):
+                        nc.tensor.matmul(
+                            turned[half][:, blocks[k]],
+                            lhsT=source[:, blocks[k]],
+                            rhs=ident[:],
+                            is_transpose=True,
+                            start=(s == 0 and k == 0),
+                            stop=(s == 1 and k == 3),
+                        )
+            if i in plan:
+                grouped = grouped_tile()
+                round_weight(grouped, waiting[i], 0)
+            for half in range(2):
+                h_t = keep.tile([P, BANK], F32, name="h_t", tag="hT%d%d" % (half, i % 2))
+                nc.scalar.copy(h_t[:], turned[half][:])
+                back.append(bank("C%d" % half))
                 for k in range(4):
-                    nc.tensor.matmul(
-                        turned[:, P * k : P * (k + 1)],
-                        lhsT=sources[s][:, P * k : P * (k + 1)],
-                        rhs=ident[:],
-                        is_transpose=True,
-                        start=(s == 0 and k == 0),
-                        stop=(s == 1 and k == 3),
-                    )
-            tag = "hT%d%d" % (half, i % 2)
-            h_t = keep.tile([P, BANK], F32, name=tag, tag=tag)
-            nc.scalar.copy(h_t[:], turned[:])
-            back = bank("C%d" % half)
-            for k in range(4):
-                nc.tensor.transpose(back[:, P * k : P * (k + 1)], h_t[:, P * k : P * (k + 1)], ident[:])
-            nc.scalar.copy(h[:, BANK * half : BANK * (half + 1)], back[:])
+                    nc.tensor.transpose(back[half][:, blocks[k]], h_t[:, blocks[k]], ident[:])
+            if i in plan:
+                round_weight(grouped, waiting[i], 1)
+                target = w1q if i < 5 else w3q
+                target[plan[i][1]] = quantize(grouped, "w_%d" % i) if i < 7 else grouped
+            for half in range(2):
+                nc.scalar.copy(h[:, halves[half]], back[half][:])
 
-        x_b = [keep.tile([P, PICKS, PACK], BF16, name="x_b%d" % a, align_bytes=64) for a in range(PASSES)]
-        xq = {}
+        xq, picked = {}, {}
+        x_t = [keep.tile([P, 4, 2, P], F32, name="x_t%d" % a) for a in range(PASSES)]
 
         def pick_x(tiles, tag):
             got = keep.tile([P, len(tiles), PICKS], F32, name="got", tag=tag)
             for n, i in enumerate(tiles):
                 nc.vector.tensor_copy(got[:, n, :], pages[i][:].indirect(idx3[:]))
-            for n, i in enumerate(tiles):
-                b, t = divmod(i, PACK)
-                nc.scalar.activation(x_b[b][:, :, t], got[:, n, :], ACT.Abs, scale=gx_t[:, b, t : t + 1])
-                if t == PACK - 1:
-                    xq[b] = quantize(x_b[b][:].rearrange("p m t -> p (m t)"), "x%d" % b)
+                picked[i] = got[:, n, :]
 
-        hs = {}
+        def magnitude(i):
+            a, c = divmod(i, PACK)
+            x_b = keep.tile([P, PICKS], BF16, name="x_b", tag="hT0%d" % ((i + 3) % 2))
+            nc.scalar.activation(x_b[:], picked[i], ACT.Abs, scale=factors[:, i : i + 1])
+            turned = bank("D0", BF16)
+            for mb in range(4):
+                nc.tensor.transpose(turned[:, blocks[mb]], x_b[:, blocks[mb]], ident_b[:])
+            nc.scalar.copy(
+                x_t[a][:, :, :, 32 * c : 32 * (c + 1)],
+                turned[:].bitcast(F32).rearrange("p (b q u) -> p b u q", b=4, u=2),
+            )
+
+        def quantize_x(a):
+            grouped = keep.tile([P, PACK * BANK], BF16, name="x_grouped", tag="x_grouped", align_bytes=64)
+            words = grouped[:].bitcast(F32).rearrange("p (h b m u) -> p h b m u", h=2, b=2, u=2)
+            for h in range(2):
+                turned = bank("D%d" % (h * a))
+                for n in range(4):
+                    nc.tensor.transpose(turned[:, blocks[n]], x_t[a][:, 2 * h + n // 2, n % 2, :], ident[:])
+                nc.scalar.copy(words[:, h, :, :, :], turned[:].rearrange("p (b u m) -> p b m u", b=2, u=2))
+            xq[a] = quantize(grouped, "x%d" % a)
+
         for i in range(TILES):
-            b, t = divmod(i, PACK)
-            hs[i] = keep.tile([P, S], F32, name="h", tag="h%d" % (i % 2))
+            h = keep.tile([P, S], F32, name="h", tag="h%d" % (i % 3), align_bytes=64)
             if i == 0:
                 for half in range(2):
-                    cols = slice(BANK * half, BANK * (half + 1))
                     acc = first_product(i, half)
-                    nc.vector.tensor_tensor(hs[i][:, cols], acc[:], dives[i][:, cols], ADD)
-                for half in range(2):
-                    cols = slice(BANK * half, BANK * (half + 1))
-                    nc.vector.tensor_tensor(
-                        pages[i][:].indirect(idx2[:, 32 * half : 32 * (half + 1)]),
-                        hs[i][:, cols],
-                        gains[t][:, cols],
-                        MULT,
-                    )
+                    nc.vector.tensor_tensor(h[:, halves[half]], acc[:], dives[i][:, halves[half]], ADD)
             else:
-                for half in range(2):
-                    add_on_tensor(i, half, hs[i])
-                if i >= 2:
-                    pick_x([i - 2] if i < TILES - 1 else [i - 2, i - 1], "hT1%d" % (i % 2))
-                nc.vector.tensor_tensor(pages[i][:].indirect(idx2[:]), hs[i][:], gains[t][:], MULT)
+                add_on_tensor(i, h)
+            if i >= 2:
+                pick_x([i - 2] if i < TILES - 1 else [i - 2, i - 1], "hT1%d" % (i % 2))
+            if i >= 3:
+                magnitude(i - 3)
+            nc.vector.tensor_tensor(pages[i][:].indirect(idx2[:]), h[:], gain[:], MULT)
+            if i == 6:
+                quantize_x(0)
             if i + 1 < TILES:
                 load_tile(i + 1)
             if i == 0:
                 idx3 = load_list(offs3, "idx3")
                 idx4 = load_list(offs4, "idx4")
-                gx_t = keep.tile([P, PASSES, PACK], F32, name="gx_t")
-                nc.sync.dma_start(gx_t[:], gx.rearrange("(b p t) -> p b t", p=P, t=PACK))
-                gb_t = keep.tile([P, PASSES, PACK], F32, name="gb_t")
-                nc.sync.dma_start(gb_t[:], gb.rearrange("(b p t) -> p b t", p=P, t=PACK))
-                for a in range(PASSES):
-                    w1q[a, 1] = quantize_weight(load_weight(w1, a, 1), "w1_%d1" % a)
-            if 3 <= i <= 6:
-                bb, a = divmod(i - 3, PASSES)
-                w3q[a, bb] = quantize_weight(load_weight(w3, a, bb), "w3_%d%d" % (a, bb))
-            if i == 4:
+                nc.sync.dma_start(factor_rows[0:TILES, :], gx.rearrange("(c p) -> c p", p=P))
+                nc.sync.dma_start(factor_rows[TILES : 2 * TILES, :], gb.rearrange("(c p) -> c p", p=P))
+            if i == 1:
+                turned = bank("D0")
+                nc.tensor.transpose(turned[:, blocks[0]], factor_rows[:], ident[:])
+                factors = keep.tile([P, 2 * TILES], F32, name="factors")
+                nc.scalar.copy(factors[:], turned[:, 0 : 2 * TILES])
+            if i == 6:
                 w2_c = keep.tile([P, PASSES, 2048], U8, name="w2_c", align_bytes=64)
                 nc.sync.dma_start(w2_c[:].bitcast(I32), w2_words.rearrange("a p c -> p a c").bitcast(I32))
                 for q in range(4):
@@ -222,100 +260,77 @@ def tile_list_tissue_page_features_kernel(
                         w2_scales[:, 4 * q : 4 * q + 4, :].rearrange("a r c -> r a c").bitcast(I32),
                     )
 
-        def y2_pass(acc, i, a):
-            b, t = divmod(i, PACK)
-            codes, scales = w3q[a, b]
-            rows = slice(P * t, P * (t + 1))
+        w3q[3] = grouped_tile()
+        for a in range(PASSES):
+            round_weight(w3q[3], waiting[TILES], a)
+        magnitude(5)
+        magnitude(6)
+
+        y2, p = {}, {}
+
+        def second_pass(acc, codes, scales, a):
             nc.tensor.matmul_mx(
                 out=acc[:],
-                lhsT=codes[:, rows].bitcast(FP8X4),
-                lhsT_scale=scales[:, rows],
-                rhs=xq[a][0][:].bitcast(FP8X4),
+                lhsT=codes,
+                lhsT_scale=scales,
+                rhs=xq[a][0].bitcast(FP8X4),
                 rhs_scale=xq[a][1][:],
                 start=(a == 0),
                 stop=(a == PASSES - 1),
             )
 
-        def p_pass(acc, b, mb, a):
-            cols = slice(P * mb, P * (mb + 1))
-            nc.tensor.matmul_mx(
-                out=acc[:],
-                lhsT=xq[a][0][:, cols].bitcast(FP8X4),
-                lhsT_scale=xq[a][1][:, cols],
-                rhs=w2_c[:, a, 2 * BANK * b : 2 * BANK * (b + 1)].bitcast(FP4X4),
-                rhs_scale=w2_s[:, a, BANK * b : BANK * (b + 1)],
-                start=(a == 0),
-                stop=(a == PASSES - 1),
-            )
+        def y2_pass(i, a):
+            if a == 0:
+                y2[i] = bank("CABD"[i % 4] + "0")
+            codes, scales = weight_columns(w3q, i, a)
+            second_pass(y2[i], codes, scales, a)
 
-        y2_tags = ["A0", "A1", "B0", "B1"]
-        y2 = {}
-        for i in range(4):
-            y2[i] = bank(y2_tags[i])
-            y2_pass(y2[i], i, 0)
-        pt = {}
-        for mb in range(2):
-            pt[0, mb] = bank("C%d" % mb)
-            p_pass(pt[0, mb], 0, mb, 0)
+        def p_pass(i, a):
+            if a == 0:
+                p[i] = bank("CABD"[i % 4] + "1")
+            second_pass(p[i], w2_c[:, a, 2 * P * i : 2 * P * (i + 1)].bitcast(FP4X4), w2_s[:, a, blocks[i]], a)
+
+        y2_pass(0, 0)
+        p_pass(0, 0)
 
         pick_x([TILES - 1], "hT10")
-        early_a = keep.tile([P, 2, PICKS], F32, name="early_a", tag="gain3")
-        early_b = keep.tile([P, 2, PICKS], F32, name="early_b", tag="h1")
-        early = [early_a[:, 0, :], early_a[:, 1, :], early_b[:, 0, :], early_b[:, 1, :]]
-        for i in range(EARLY):
-            nc.vector.tensor_copy(early[i], pages[i][:].indirect(idx4[:]))
+        late_codes = keep.tile([P, 2, BANK], U32, name="late_codes", tag="h1", align_bytes=64)
+        for g in range(2):
+            w3q[2 + g] = quantize(w3q[2 + g], "w3_late%d" % g, late_codes[:, g, :])
+        early = keep.tile([P, EARLY - 1, PICKS], F32, name="early", tag="gain")
+        for i in range(EARLY - 1):
+            nc.vector.tensor_copy(early[:, i, :], pages[i][:].indirect(idx4[:]))
+        magnitude(TILES - 1)
+        quantize_x(1)
+        last = keep.tile([P, PICKS], F32, name="last", tag="x_grouped", align_bytes=64)
+        nc.vector.tensor_copy(last[:], pages[EARLY - 1][:].indirect(idx4[:]))
+        buddies = [early[:, i, :] for i in range(EARLY - 1)] + [last[:]]
 
-        z = {}
+        z_all = [ring.tile([P, PACK, PICKS], F32, name="z_all", tag="raw") for n in range(2)]
+        y_all = [keep.tile([P, PACK, PICKS], F32, name="y_all", tag="tab%d" % n) for n in range(2)]
+        z = [z_all[i // PACK][:, i % PACK, :] for i in range(TILES)]
+        y = [y_all[i // PACK][:, i % PACK, :] for i in range(TILES)]
 
-        def buddy(i):
-            b, t = divmod(i, PACK)
-            z[i] = ring.tile([P, PICKS], F32, name="z", tag="z", bufs=6)
+        def buddy_product(i):
+            for a in range(1 if i == 0 else 0, PASSES):
+                y2_pass(i, a)
+            gb_i = factors[:, TILES + i : TILES + i + 1]
             if i < EARLY:
-                nc.vector.scalar_tensor_tensor(z[i][:], y2[i][:], gb_t[:, b, t : t + 1], early[i], MULT, MULT)
+                nc.vector.scalar_tensor_tensor(z[i], y2[i][:], gb_i, buddies[i], MULT, MULT)
             else:
-                scaled = ring.tile([P, PICKS], F32, name="scaled", tag="dive", bufs=3)
-                nc.scalar.activation(scaled[:], y2[i][:], ACT.Copy, scale=gb_t[:, b, t : t + 1])
-                nc.vector.tensor_tensor(z[i][:], pages[i][:].indirect(idx4[:]), scaled[:], MULT)
-
-        y_t = [keep.tile([P, 4, PACK, P], F32, name="y_t%d" % b, tag="tab%d" % b) for b in range(2)]
-
-        def silu(b, mb):
-            nc.scalar.activation(y_t[b][:, mb, :, :], pt[b, mb][:].rearrange("p (q t) -> p t q", t=PACK), ACT.Silu)
-
-        def p_whole(b, mb):
-            pt[b, mb] = bank("C%d" % (mb % 2))
-            for a in range(PASSES):
-                p_pass(pt[b, mb], b, mb, a)
-            silu(b, mb)
-
-        def y2_whole(i):
-            y2[i] = bank(y2_tags[i % 4])
-            for a in range(PASSES):
-                y2_pass(y2[i], i, a)
-            buddy(i)
+                scaled = ring.tile([P, PICKS], F32, name="scaled", tag="dive")
+                nc.scalar.activation(scaled[:], y2[i][:], ACT.Copy, scale=gb_i)
+                nc.vector.tensor_tensor(z[i], pages[i][:].indirect(idx4[:]), scaled[:], MULT)
 
         def finish(i):
-            b, t = divmod(i, PACK)
-            y = bank("D%d" % (i % 2))
-            for mb in range(4):
-                nc.tensor.transpose(y[:, P * mb : P * (mb + 1)], y_t[b][:, mb, t, :], ident[:])
-            nc.vector.tensor_tensor(z[i][:], y[:], z[i][:], ADD)
-            nc.sync.dma_start(dealt(out)[b, t], z[i][:])
+            for a in range(1 if i == 0 else 0, PASSES):
+                p_pass(i, a)
+            nc.scalar.activation(y[i], p[i][:], ACT.Silu)
+            nc.vector.tensor_tensor(z[i], z[i], y[i], ADD)
+            nc.sync.dma_start(out[blocks[i], :], z[i])
 
-        for i in range(4):
-            y2_pass(y2[i], i, 1)
-            buddy(i)
-        for mb in range(2):
-            p_pass(pt[0, mb], 0, mb, 1)
-            silu(0, mb)
-        for mb in range(2, 4):
-            p_whole(0, mb)
-        for i in range(4, 6):
-            y2_whole(i)
-        for mb in range(4):
-            p_whole(1, mb)
-            finish(mb)
-            if mb < 2:
-                y2_whole(6 + mb)
-        for i in range(4, TILES):
+        buddy_product(0)
+        for i in range(TILES):
+            if i + 1 < TILES:
+                buddy_product(i + 1)
             finish(i)

from contextlib import ExitStack

import concourse.mybir as mybir
from concourse.masks import make_identity

FLOPS = 4294967296

F32 = mybir.dt.float32
BF16 = mybir.dt.bfloat16
I32 = mybir.dt.int32
U32 = mybir.dt.uint32
U16 = mybir.dt.uint16
U8 = mybir.dt.uint8
FP8X4 = mybir.dt.float8_e4m3fn_x4
FP4X4 = mybir.dt.float4_e2m1fn_x4
ACT = mybir.ActivationFunctionType
MULT = mybir.AluOpType.mult
ADD = mybir.AluOpType.add

P = 128
PACK = 4
BANK = 512
PASSES = 2
TILES = 8
T = 2048
S = 1024
PICKS = 512
WIDE = 256
EARLY = 4


def tile_list_tissue_page_features_kernel(
    tc, tab_words, tab_scales, offs, offs2, offs3, offs4, w1, dive, wgs, page0, gx, w2_words, w2_scales, w3, gb, out
):
    nc = tc.nc
    with ExitStack() as ctx:
        keep = ctx.enter_context(tc.tile_pool(name="keep", bufs=1))
        ring = ctx.enter_context(tc.tile_pool(name="ring", bufs=3))
        psum = ctx.enter_context(tc.psum_pool(name="psum", bufs=1))

        halves = [slice(BANK * n, BANK * (n + 1)) for n in range(2)]
        blocks = [slice(P * n, P * (n + 1)) for n in range(TILES)]

        def bank(tag, dtype=F32):
            return psum.tile([P, BANK], dtype, name=tag, tag=tag)

        tab_s = keep.tile([P, T], U8, name="tab_s")
        nc.gpsimd.memset(tab_s[:].bitcast(I32), 0)
        warm = keep.tile([P, 8], F32, name="warm")
        nc.gpsimd.memset(warm[:], 0.0)
        warm_out = keep.tile([P, 8], F32, name="warm_out")
        nc.scalar.activation(warm_out[:], warm[:], ACT.Silu)
        w2_s = keep.tile([P, PASSES, 1024], U8, name="w2_s", align_bytes=64)
        nc.gpsimd.memset(w2_s[:].rearrange("p a c -> p (a c)").bitcast(I32), 0)
        factor_rows = keep.tile([P, P], F32, name="factor_rows")
        nc.gpsimd.memset(factor_rows[:], 0.0)
        ident = keep.tile([P, P], F32, name="ident")
        make_identity(nc, ident[:])
        ident_b = keep.tile([P, P], BF16, name="ident_b")
        make_identity(nc, ident_b[:])

        def load_list(x, name):
            t = keep.tile([P, x.shape[1]], U16, name=name)
            nc.sync.dma_start(t[:], x)
            return t

        def load_table(a):
            t = keep.tile([P, T], I32, name="tab%d" % a, tag="tab%d" % a)
            nc.sync.dma_start(t[:], tab_words[a].rearrange("p t i -> p (t i)").bitcast(I32))
            return t

        def raw_tile():
            return ring.tile([P, PASSES, PACK, WIDE], F32, name="raw", tag="raw")

        def load_weight(raw, w, g, a):
            rows = w[BANK * a : BANK * (a + 1), WIDE * g : WIDE * (g + 1)]
            nc.sync.dma_start(raw[:, a, :, :], rows.rearrange("(p j) c -> p j c", j=PACK))

        def grouped_tile():
            return ring.tile([P, PACK * BANK], BF16, name="grouped", tag="grouped", align_bytes=64)

        def round_weight(grouped, raw, a):
            dst = grouped[:].rearrange("p (a c i j) -> p a c j i", a=PASSES, i=4, j=PACK)
            src = raw[:].rearrange("p a j (c i) -> p a c j i", i=4)
            nc.scalar.copy(dst[:, a, :, :, :], src[:, a, :, :, :])

        def quantize(grouped, name, codes=None):
            if codes is None:
                codes = keep.tile([P, BANK], U32, name=name + "_c", align_bytes=64)[:]
            scales = keep.tile([P, BANK], U8, name=name + "_s", align_bytes=64)
            nc.vector.quantize_mx(out=codes.bitcast(FP8X4), scales=scales[:], in_=grouped[:])
            return codes, scales

        def weight_columns(q, i, a):
            codes, scales = q[i // 2]
            cols = slice(WIDE * a + P * (i % 2), WIDE * a + P * (i % 2 + 1))
            return codes[:, cols].bitcast(FP8X4), scales[:, cols]

        pages, dives, waiting = {}, {}, {}
        plan = {1: (w1, 1), 3: (w1, 2), 4: (w1, 3), 5: (w3, 0), 6: (w3, 1), 7: (w3, 2), 8: (w3, 3)}

        def load_tile(i):
            early = i in plan and i < 5
            if early:
                waiting[i] = raw_tile()
                load_weight(waiting[i], w1, plan[i][1], 0)
            dives[i] = ring.tile([P, S], F32, name="dive", tag="dive")
            nc.sync.dma_start(dives[i][:], dive[blocks[i], :])
            if early:
                load_weight(waiting[i], w1, plan[i][1], 1)
            if i == 0:
                nc.sync.dma_start(gain[:], wgs)
            pages[i] = keep.tile([P, T], F32, name="page%d" % i)
            nc.sync.dma_start(pages[i][:], page0[blocks[i], :])
            if i >= 4:
                waiting[i + 1] = raw_tile()
                for a in range(PASSES):
                    load_weight(waiting[i + 1], w3, i - 4, a)

        idx = load_list(offs, "idx")
        tabs = [load_table(0)]
        for q in range(4):
            nc.sync.dma_start(
                tab_s[32 * q : 32 * q + 8, :].bitcast(I32), tab_scales[:, 4 * q : 4 * q + 4, :].bitcast(I32)
            )
        raw = raw_tile()
        for a in range(PASSES):
            load_weight(raw, w1, 0, a)
        tabs.append(load_table(1))
        idx2 = load_list(offs2, "idx2")
        gain = keep.tile([P, S], F32, name="gain", tag="gain")
        load_tile(0)

        v_c = [keep.tile([P, S], U32, name="v_c%d" % a, align_bytes=64) for a in range(PASSES)]
        v_s = keep.tile([P, S], U8, name="v_s", align_bytes=64)
        w1q, w3q = {}, {}
        nc.vector.tensor_copy(v_c[0][:], tabs[0][:].bitcast(U32).indirect(idx[:]))
        nc.vector.tensor_copy(v_s[:], tab_s[:].indirect(idx[:]))
        grouped = grouped_tile()
        for a in range(PASSES):
            round_weight(grouped, raw, a)
        w1q[0] = quantize(grouped, "w1_0")
        for half in range(2):
            nc.vector.tensor_copy(
                v_c[1][:, halves[half]], tabs[1][:].bitcast(U32).indirect(idx[:, 32 * half : 32 * (half + 1)])
            )

        def first_product(i, half):
            acc = bank(("A%d" if i > 0 else "C%d") % half)
            for a in range(PASSES):
                codes, scales = weight_columns(w1q, i, a)
                nc.tensor.matmul_mx(
                    out=acc[:],
                    lhsT=codes,
                    lhsT_scale=scales,
                    rhs=v_c[a][:, halves[half]].bitcast(FP8X4),
                    rhs_scale=v_s[4 * a : P, halves[half]],
                    start=(a == 0),
                    stop=(a == PASSES - 1),
                )
            return acc

        def add_on_tensor(i, h):
            turned, back = [], []
            for half in range(2):
                acc = first_product(i, half)
                prod = ring.tile([P, BANK], F32, name="prod", tag="prod", bufs=2)
                nc.scalar.copy(prod[:], acc[:])
                turned.append(bank(["B0", "B1", "D1"][(2 * i + half) % 3]))
                for s, source in enumerate([dives[i][:, halves[half]], prod[:]]):
                    for k in range(4):
                        nc.tensor.matmul(
                            turned[half][:, blocks[k]],
                            lhsT=source[:, blocks[k]],
                            rhs=ident[:],
                            is_transpose=True,
                            start=(s == 0 and k == 0),
                            stop=(s == 1 and k == 3),
                        )
            if i in plan:
                grouped = grouped_tile()
                round_weight(grouped, waiting[i], 0)
            for half in range(2):
                h_t = keep.tile([P, BANK], F32, name="h_t", tag="hT%d%d" % (half, i % 2))
                nc.scalar.copy(h_t[:], turned[half][:])
                back.append(bank("C%d" % half))
                for k in range(4):
                    nc.tensor.transpose(back[half][:, blocks[k]], h_t[:, blocks[k]], ident[:])
            if i in plan:
                round_weight(grouped, waiting[i], 1)
                target = w1q if i < 5 else w3q
                target[plan[i][1]] = quantize(grouped, "w_%d" % i) if i < 7 else grouped
            for half in range(2):
                nc.scalar.copy(h[:, halves[half]], back[half][:])

        xq, picked = {}, {}
        x_t = [keep.tile([P, 4, 2, P], F32, name="x_t%d" % a) for a in range(PASSES)]

        def pick_x(tiles, tag):
            got = keep.tile([P, len(tiles), PICKS], F32, name="got", tag=tag)
            for n, i in enumerate(tiles):
                nc.vector.tensor_copy(got[:, n, :], pages[i][:].indirect(idx3[:]))
                picked[i] = got[:, n, :]

        def magnitude(i):
            a, c = divmod(i, PACK)
            x_b = keep.tile([P, PICKS], BF16, name="x_b", tag="hT0%d" % ((i + 3) % 2))
            nc.scalar.activation(x_b[:], picked[i], ACT.Abs, scale=factors[:, i : i + 1])
            turned = bank("D0", BF16)
            for mb in range(4):
                nc.tensor.transpose(turned[:, blocks[mb]], x_b[:, blocks[mb]], ident_b[:])
            nc.scalar.copy(
                x_t[a][:, :, :, 32 * c : 32 * (c + 1)],
                turned[:].bitcast(F32).rearrange("p (b q u) -> p b u q", b=4, u=2),
            )

        def quantize_x(a):
            grouped = keep.tile([P, PACK * BANK], BF16, name="x_grouped", tag="x_grouped", align_bytes=64)
            words = grouped[:].bitcast(F32).rearrange("p (h b m u) -> p h b m u", h=2, b=2, u=2)
            for h in range(2):
                turned = bank("D%d" % (h * a))
                for n in range(4):
                    nc.tensor.transpose(turned[:, blocks[n]], x_t[a][:, 2 * h + n // 2, n % 2, :], ident[:])
                nc.scalar.copy(words[:, h, :, :, :], turned[:].rearrange("p (b u m) -> p b m u", b=2, u=2))
            xq[a] = quantize(grouped, "x%d" % a)

        for i in range(TILES):
            h = keep.tile([P, S], F32, name="h", tag="h%d" % (i % 3), align_bytes=64)
            if i == 0:
                for half in range(2):
                    acc = first_product(i, half)
                    nc.vector.tensor_tensor(h[:, halves[half]], acc[:], dives[i][:, halves[half]], ADD)
            else:
                add_on_tensor(i, h)
            if i >= 2:
                pick_x([i - 2] if i < TILES - 1 else [i - 2, i - 1], "hT1%d" % (i % 2))
            if i >= 3:
                magnitude(i - 3)
            nc.vector.tensor_tensor(pages[i][:].indirect(idx2[:]), h[:], gain[:], MULT)
            if i == 6:
                quantize_x(0)
            if i + 1 < TILES:
                load_tile(i + 1)
            if i == 0:
                idx3 = load_list(offs3, "idx3")
                idx4 = load_list(offs4, "idx4")
                nc.sync.dma_start(factor_rows[0:TILES, :], gx.rearrange("(c p) -> c p", p=P))
                nc.sync.dma_start(factor_rows[TILES : 2 * TILES, :], gb.rearrange("(c p) -> c p", p=P))
            if i == 1:
                turned = bank("D0")
                nc.tensor.transpose(turned[:, blocks[0]], factor_rows[:], ident[:])
                factors = keep.tile([P, 2 * TILES], F32, name="factors")
                nc.scalar.copy(factors[:], turned[:, 0 : 2 * TILES])
            if i == 6:
                w2_c = keep.tile([P, PASSES, 2048], U8, name="w2_c", align_bytes=64)
                nc.sync.dma_start(w2_c[:].bitcast(I32), w2_words.rearrange("a p c -> p a c").bitcast(I32))
                for q in range(4):
                    nc.sync.dma_start(
                        w2_s[32 * q : 32 * q + 4, :, :].bitcast(I32),
                        w2_scales[:, 4 * q : 4 * q + 4, :].rearrange("a r c -> r a c").bitcast(I32),
                    )

        w3q[3] = grouped_tile()
        for a in range(PASSES):
            round_weight(w3q[3], waiting[TILES], a)
        magnitude(5)
        magnitude(6)

        y2, p = {}, {}

        def second_pass(acc, codes, scales, a):
            nc.tensor.matmul_mx(
                out=acc[:],
                lhsT=codes,
                lhsT_scale=scales,
                rhs=xq[a][0].bitcast(FP8X4),
                rhs_scale=xq[a][1][:],
                start=(a == 0),
                stop=(a == PASSES - 1),
            )

        def y2_pass(i, a):
            if a == 0:
                y2[i] = bank("CABD"[i % 4] + "0")
            codes, scales = weight_columns(w3q, i, a)
            second_pass(y2[i], codes, scales, a)

        def p_pass(i, a):
            if a == 0:
                p[i] = bank("CABD"[i % 4] + "1")
            second_pass(p[i], w2_c[:, a, 2 * P * i : 2 * P * (i + 1)].bitcast(FP4X4), w2_s[:, a, blocks[i]], a)

        y2_pass(0, 0)
        p_pass(0, 0)

        pick_x([TILES - 1], "hT10")
        late_codes = keep.tile([P, 2, BANK], U32, name="late_codes", tag="h1", align_bytes=64)
        for g in range(2):
            w3q[2 + g] = quantize(w3q[2 + g], "w3_late%d" % g, late_codes[:, g, :])
        early = keep.tile([P, EARLY - 1, PICKS], F32, name="early", tag="gain")
        for i in range(EARLY - 1):
            nc.vector.tensor_copy(early[:, i, :], pages[i][:].indirect(idx4[:]))
        magnitude(TILES - 1)
        quantize_x(1)
        last = keep.tile([P, PICKS], F32, name="last", tag="x_grouped", align_bytes=64)
        nc.vector.tensor_copy(last[:], pages[EARLY - 1][:].indirect(idx4[:]))
        buddies = [early[:, i, :] for i in range(EARLY - 1)] + [last[:]]

        z_all = [ring.tile([P, PACK, PICKS], F32, name="z_all", tag="raw") for n in range(2)]
        y_all = [keep.tile([P, PACK, PICKS], F32, name="y_all", tag="tab%d" % n) for n in range(2)]
        z = [z_all[i // PACK][:, i % PACK, :] for i in range(TILES)]
        y = [y_all[i // PACK][:, i % PACK, :] for i in range(TILES)]

        def buddy_product(i):
            for a in range(1 if i == 0 else 0, PASSES):
                y2_pass(i, a)
            gb_i = factors[:, TILES + i : TILES + i + 1]
            if i < EARLY:
                nc.vector.scalar_tensor_tensor(z[i], y2[i][:], gb_i, buddies[i], MULT, MULT)
            else:
                scaled = ring.tile([P, PICKS], F32, name="scaled", tag="dive")
                nc.scalar.activation(scaled[:], y2[i][:], ACT.Copy, scale=gb_i)
                nc.vector.tensor_tensor(z[i], pages[i][:].indirect(idx4[:]), scaled[:], MULT)

        def finish(i):
            for a in range(1 if i == 0 else 0, PASSES):
                p_pass(i, a)
            nc.scalar.activation(y[i], p[i][:], ACT.Silu)
            nc.vector.tensor_tensor(z[i], z[i], y[i], ADD)
            nc.sync.dma_start(out[blocks[i], :], z[i])

        buddy_product(0)
        for i in range(TILES):
            if i + 1 < TILES:
                buddy_product(i + 1)
            finish(i)
